import numpy as np
import ml_dtypes


def mxq(x, axis, fmt="e4m3"):
    dtype, down = {"e4m3": (ml_dtypes.float8_e4m3fn, 7), "e5m2": (ml_dtypes.float8_e5m2, 14)}[fmt]
    v = np.moveaxis(np.asarray(x, np.float32).astype(ml_dtypes.bfloat16).astype(np.float64), axis, -1)
    blocks = v.reshape(v.shape[:-1] + (-1, 32))
    amax = np.abs(blocks).max(-1, keepdims=True)
    byte = np.maximum(np.where(amax > 0, np.frexp(amax)[1] - 1 + 127, 0) - down, 1)
    scale = np.exp2(byte - 127.0)
    codes = (blocks / scale).astype(np.float32).astype(dtype).astype(np.float64)
    return np.moveaxis((codes * scale).reshape(v.shape), -1, axis)


WIDE = False


def mx_kscale(k):
    if not WIDE:
        return np.ones(k)
    levels = np.array([10, -10, 5, -5, 0])
    if k % 512:
        return np.exp2(np.random.permutation(np.resize(levels, k // 32))).repeat(32)
    a = np.empty((k // 512, 16))
    for p in range(k // 512):
        a[p, :8] = np.random.permutation(np.resize(levels, 8))
        for g in range(8):
            far = levels[np.abs(levels - a[p, g]) >= 10]
            a[p, g + 8] = far[np.random.randint(len(far))]
    return np.exp2(a.ravel()).repeat(32)


BF16 = ml_dtypes.bfloat16


def bf(x):
    return np.asarray(x, np.float32).astype(BF16)


def f64(x):
    return np.asarray(x).astype(np.float64)

def planes(Y):
    n, m = Y.shape
    b = f64(bf(Y)).reshape(n // 32, 32, m)
    amax = np.abs(b).max(1)
    byte = np.clip(np.where(amax > 0, np.frexp(amax)[1] - 1 + 127 - 7, 1), 1, 254)
    codes = (b * np.exp2(127.0 - byte)[:, None, :]).reshape(n, m).astype(np.float32).astype(ml_dtypes.float8_e4m3fn).view(np.uint8)
    words = codes.reshape(n // 512, 128, 4, m).transpose(0, 1, 3, 2)
    return np.ascontiguousarray(words), np.ascontiguousarray(byte.astype(np.uint8).reshape(n // 512, 16, m))


FRAMES, CH, UNITS = 2048, 1024, 1024
KEEP = 0.9
SPREAD = 0.7


def setup_inputs():
    s = mx_kscale(CH)
    unit_size = np.exp(SPREAD * np.random.randn(UNITS))
    states = np.random.randn(FRAMES, CH) / s[None, :]
    prenet_w = np.random.randn(CH, UNITS) / np.sqrt(CH) * unit_size[None, :] * s[:, None]
    prenet_b = 0.5 * np.random.randn(UNITS) * unit_size
    slope = np.random.uniform(0.25, 0.6, UNITS)
    drop_mask = np.where(np.random.rand(UNITS, FRAMES) < KEEP, 1.0 / KEEP, 0.0)
    return {"states": bf(states), "prenet_w": bf(prenet_w), "prenet_b": bf(prenet_b),
            "slope": bf(slope), "drop_mask": bf(drop_mask)}


def reference(states, prenet_w, prenet_b, slope, drop_mask):
    x = mxq(f64(states), 1, "e4m3")
    w = mxq(f64(prenet_w), 0, "e4m3")
    z = (w.T @ x.T) + f64(prenet_b)[:, None]
    y = np.maximum(z, f64(slope)[:, None] * z) * f64(drop_mask)
    Y = y.reshape(UNITS, FRAMES)
    words, scales = planes(Y)
    return y, words, scales

@@ -1,0 +1,344 @@
+from contextlib import ExitStack
+
+import concourse.mybir as mybir
+from concourse.masks import make_identity
+
+FRAMES, CH, UNITS = 2048, 1024, 1024
+FLOPS = 2 * FRAMES * CH * UNITS
+
+F32 = mybir.dt.float32
+BF16 = mybir.dt.bfloat16
+I32 = mybir.dt.int32
+U32 = mybir.dt.uint32
+U8 = mybir.dt.uint8
+FP8X4 = mybir.dt.float8_e4m3fn_x4
+ALU = mybir.AluOpType
+ACT = mybir.ActivationFunctionType
+
+P = 128
+PACK = 4
+SPAN = P * PACK
+PASSES = CH // SPAN
+GROUPS = UNITS // SPAN
+CHUNK = 512
+BLOCK = 256
+STEPS = [(0, 0, 256), (0, 256, 256), (1, 0, 512), (0, 512, 512), (1, 512, 512),
+         (0, 1024, 512), (1, 1024, 512), (0, 1536, 512), (1, 1536, 512)]
+SHARED = [2, 3, 4, 5, 6, 7, 8]
+W_SPLIT = 40
+W_SPLIT2 = 44
+Y_SPLIT = 160
+FINE = 5
+
+
+def tile_vocoder_prenet_units_first_g2_kernel(
+    tc, states, prenet_w, prenet_b, slope, drop_mask, out_0, out_1, out_2
+):
+    nc = tc.nc
+    with ExitStack() as ctx:
+        keep = ctx.enter_context(tc.tile_pool(name="keep", bufs=1))
+        stage = ctx.enter_context(tc.tile_pool(name="stage", bufs=2))
+        turn_psum = ctx.enter_context(tc.psum_pool(name="turn_psum", bufs=3))
+        acc_psum = ctx.enter_context(tc.psum_pool(name="acc_psum", bufs=5))
+        ctx.enter_context(tc.manual_schedule())
+
+        w_raw, x_raw, masks_held = {}, {}, []
+
+        def load_w(c, g):
+            w_raw[c, g] = keep.tile([P, PACK, SPAN], BF16, name="w_raw_%d_%d" % (c, g))
+            rows = prenet_w[c * SPAN : (c + 1) * SPAN, g * SPAN : (g + 1) * SPAN]
+            nc.sync.dma_start(out=w_raw[c, g][:], in_=rows.rearrange("(p j) u -> p j u", j=PACK))
+
+        def load_x(b):
+            x_raw[b] = keep.tile([P, 2 * CH], BF16, name="x_raw_%d" % b)
+            rows = states[b * BLOCK : (b + 1) * BLOCK, :]
+            nc.sync.dma_start(out=x_raw[b][:], in_=rows.rearrange("(r i) k -> r (i k)", i=2))
+
+        def load_mask(g, first, count):
+            held = keep.tile([P, PACK, count], BF16, name="mask_%d_%d" % (g, first))
+            rows = drop_mask[g * SPAN : (g + 1) * SPAN, first : first + count]
+            nc.sync.dma_start(out=held[:], in_=rows.rearrange("(p t) f -> p t f", t=PACK))
+            masks_held.append((g, first, count, held))
+
+        def mask_of(s, t):
+            g, f0, n = STEPS[s]
+            for group, first, count, held in masks_held:
+                if group == g and first <= f0 < first + count:
+                    return held[:, t, f0 - first : f0 - first + n]
+            raise ValueError("no mask tile")
+
+        bias = keep.tile([P, GROUPS, PACK], BF16, name="bias")
+        leak = keep.tile([P, GROUPS, PACK], BF16, name="leak")
+
+        load_w(0, 0)
+        load_x(0)
+        load_w(1, 0)
+        nc.sync.dma_start(out=bias[:], in_=prenet_b.rearrange("(g p t) -> p g t", p=P, t=PACK))
+        nc.sync.dma_start(out=leak[:], in_=slope.rearrange("(g p t) -> p g t", p=P, t=PACK))
+        load_x(1)
+        load_mask(0, 0, 512)
+        load_w(0, 1)
+        load_x(2)
+        load_w(1, 1)
+        load_x(3)
+        load_mask(1, 0, 512)
+        load_mask(0, 512, 512)
+        load_mask(1, 512, 512)
+        load_x(4)
+        load_x(5)
+        load_mask(0, 1024, 1024)
+        load_x(6)
+        load_x(7)
+        load_mask(1, 1024, 1024)
+
+        ident = keep.tile([P, P], F32, name="ident")
+        make_identity(nc, ident[:])
+
+        w_grouped, w_codes, w_scales = {}, {}, {}
+        x_grouped, x_codes, x_scales = {}, {}, {}
+        acc, y, y_grouped, low, whole = {}, {}, {}, {}, {}
+        y_scales = keep.tile([P, FRAMES], U8, name="y_scales", align_bytes=64)
+
+        def group_w(c, g, copy, lo=0, hi=P // 2):
+            if (c, g) not in w_grouped:
+                w_grouped[c, g] = stage.tile([P, PACK * SPAN], BF16, name="w_grouped", align_bytes=64)
+            copy(
+                out=w_grouped[c, g][:].rearrange("p (t m n j) -> p m t n j", t=PACK, n=2, j=PACK)[:, lo:hi],
+                in_=w_raw[c, g][:].rearrange("p j (m n t) -> p m t n j", n=2, t=PACK)[:, lo:hi],
+            )
+
+        def quantize_w(c, g):
+            w_codes[c, g] = keep.tile([P, SPAN], U32, name="w_codes_%d_%d" % (c, g), align_bytes=64)
+            w_scales[c, g] = keep.tile([P, SPAN], U8, name="w_scales_%d_%d" % (c, g), align_bytes=64)
+            nc.vector.quantize_mx(
+                out=w_codes[c, g][:].bitcast(FP8X4), scales=w_scales[c, g][:], in_=w_grouped[c, g][:]
+            )
+
+        turned = {}
+
+        def turn_x(b, c):
+            turned[b, c] = turn_psum.tile([P, 4, P], F32, name="turned")
+            words = x_raw[b][:].bitcast(F32)
+            for i in range(2):
+                for u in range(2):
+                    first = i * (CH // 2) + c * (SPAN // 2)
+                    nc.tensor.transpose(
+                        turned[b, c][:, 2 * i + u, :], words[:, first + u : first + SPAN // 2 : 2], ident[:]
+                    )
+
+        def group_x(b, c):
+            f, half = divmod(b, 2)
+            if half == 0:
+                x_grouped[f, c] = stage.tile([P, PACK * CHUNK], BF16, name="x_grouped", bufs=3, align_bytes=64)
+            words = x_grouped[f, c][:].bitcast(F32)[:, half * 2 * BLOCK : (half + 1) * 2 * BLOCK]
+            nc.scalar.copy(
+                out=words.rearrange("p (r q) -> p r q", q=4), in_=turned[b, c][:].rearrange("p q r -> p r q")
+            )
+
+        def prepare_x(b, c):
+            turn_x(b, c)
+            group_x(b, c)
+
+        def quantize_x(f, c, lo=0, hi=CHUNK):
+            if (f, c) not in x_codes:
+                x_codes[f, c] = keep.tile([P, CHUNK], U32, name="x_codes_%d_%d" % (f, c), align_bytes=64)
+                x_scales[f, c] = keep.tile([P, CHUNK], U8, name="x_scales_%d_%d" % (f, c), align_bytes=64)
+            nc.vector.quantize_mx(
+                out=x_codes[f, c][:, lo:hi].bitcast(FP8X4), scales=x_scales[f, c][:, lo:hi],
+                in_=x_grouped[f, c][:, PACK * lo : PACK * hi],
+            )
+
+        def multiply(s, t):
+            g, f0, n = STEPS[s]
+            f, lo = divmod(f0, CHUNK)
+            acc[s, t] = acc_psum.tile([P, n], F32, name="acc")
+            cols = slice(t * P, (t + 1) * P)
+            for c in range(PASSES):
+                nc.tensor.matmul_mx(
+                    out=acc[s, t][:],
+                    lhsT=w_codes[c, g][:, cols].bitcast(FP8X4),
+                    lhsT_scale=w_scales[c, g][:, cols],
+                    rhs=x_codes[f, c][:, lo : lo + n].bitcast(FP8X4),
+                    rhs_scale=x_scales[f, c][:, lo : lo + n],
+                    start=(c == 0),
+                    stop=(c == PASSES - 1),
+                )
+            if t == 0 and s in SHARED:
+                low[s] = stage.tile([P, CHUNK], F32, name="low")
+                nc.scalar.activation(
+                    out=low[s][:, :n], in_=acc[s, t][:], func=ACT.Identity,
+                    scale=leak_f32[:, g : g + 1], bias=leak_bias[:, g : g + 1],
+                )
+
+        def read_acc(s, t):
+            g, f0, n = STEPS[s]
+            if t == 0 and s != 1:
+                whole[s] = keep.tile([P, PACK, CHUNK], F32, name="y_%d" % s)
+                y[s] = whole[s][:, :, :n]
+            if t == 0 and s == 1:
+                whole[1] = whole[0]
+                y[1] = whole[1][:, :, BLOCK:]
+            if t == 0 and s in SHARED:
+                nc.vector.scalar_tensor_tensor(
+                    out=low[s][:, :n], in0=acc[s, t][:], scalar=bias[:, g, t : t + 1], in1=low[s][:, :n],
+                    op0=ALU.add, op1=ALU.max,
+                )
+                nc.gpsimd.tensor_tensor(out=y[s][:, t, :], in0=low[s][:, :n], in1=mask_of(s, t), op=ALU.mult)
+            else:
+                nc.vector.scalar_tensor_tensor(
+                    out=y[s][:, t, :], in0=acc[s, t][:], scalar=bias[:, g, t : t + 1], in1=mask_of(s, t),
+                    op0=ALU.add, op1=ALU.mult,
+                )
+
+        def rectify(s, t):
+            g, f0, n = STEPS[s]
+            if not (t == 0 and s in SHARED):
+                nc.vector.scalar_tensor_tensor(
+                    out=y[s][:, t, :], in0=y[s][:, t, :], scalar=leak[:, g, t : t + 1], in1=y[s][:, t, :],
+                    op0=ALU.mult, op1=ALU.max,
+                )
+
+        def store_y(s, lo=0, hi=PACK):
+            g, f0, n = STEPS[s]
+            f0 = f0 // CHUNK * CHUNK
+            rows = out_0[g * SPAN : (g + 1) * SPAN, f0 : f0 + CHUNK]
+            nc.sync.dma_start(out=rows.rearrange("(p t) f -> p t f", t=PACK)[:, lo:hi, :], in_=whole[s][:, lo:hi, :])
+
+        def group_y(s, copy, lo=0, hi=CHUNK // 2):
+            if s not in y_grouped:
+                y_grouped[s] = stage.tile([P, PACK * CHUNK], BF16, name="y_grouped", align_bytes=64)
+            copy(
+                out=y_grouped[s][:].rearrange("p (c i t) -> p c t i", i=2, t=PACK)[:, lo:hi],
+                in_=whole[s][:].rearrange("p t (c i) -> p c t i", i=2)[:, lo:hi],
+            )
+
+        def quantize_y(s):
+            g, f0, n = STEPS[s]
+            f0 = f0 // CHUNK * CHUNK
+            cols = slice(f0, f0 + CHUNK)
+            y_codes = keep.tile([P, CHUNK], U32, name="y_codes_%d" % s, align_bytes=64)
+            nc.vector.quantize_mx(out=y_codes[:].bitcast(FP8X4), scales=y_scales[4 * g :, cols], in_=y_grouped[s][:])
+            nc.sync.dma_start(
+                out=out_1[g, :, cols, :].rearrange("p m t -> p (m t)").bitcast(I32), in_=y_codes[:].bitcast(I32)
+            )
+
+        def store_scales():
+            for q in range(4):
+                queue = nc.scalar if q % 2 == 0 else nc.sync
+                queue.dma_start(
+                    out=out_2[:, 4 * q : 4 * q + 4, :].bitcast(I32),
+                    in_=y_scales[32 * q : 32 * q + 4 * GROUPS, :].bitcast(I32),
+                )
+
+        if SHARED:
+            warm = keep.tile([P, 1], F32, name="warm")
+            nc.scalar.activation(out=warm[:], in_=ident[:, 0:1], func=ACT.Identity)
+        group_w(0, 0, nc.vector.tensor_copy)
+        quantize_w(0, 0)
+        prepare_x(0, 0)
+        group_w(1, 0, nc.vector.tensor_copy, 0, W_SPLIT)
+        group_w(1, 0, nc.scalar.copy, W_SPLIT, P // 2)
+        prepare_x(0, 1)
+        quantize_x(0, 0, 0, BLOCK)
+        quantize_w(1, 0)
+        quantize_x(0, 1, 0, BLOCK)
+        if SHARED:
+            leak_f32 = keep.tile([P, GROUPS], F32, name="leak_f32")
+            leak_bias = keep.tile([P, GROUPS], F32, name="leak_bias")
+            nc.gpsimd.tensor_copy(out=leak_f32[:], in_=leak[:, :, 0])
+            nc.gpsimd.tensor_tensor(out=leak_bias[:], in0=leak[:, :, 0], in1=bias[:, :, 0], op=ALU.mult)
+        prepare_x(1, 0)
+        for t in range(PACK):
+            multiply(0, t)
+        last = len(STEPS) - 1
+
+        def reads(s, between):
+            multiply(s + 1, 0)
+            for t in range(PACK):
+                read_acc(s, t)
+                if t < len(between):
+                    prepare_x(*between[t])
+                if t + 1 < PACK:
+                    multiply(s + 1, t + 1)
+
+        def rectify_all(s):
+            if s >= FINE and s in SHARED:
+                store_y(s, 0, 1)
+            for t in range(PACK):
+                rectify(s, t)
+                if s >= FINE and not (t == 0 and s in SHARED):
+                    store_y(s, t, t + 1)
+            if s < FINE:
+                store_y(s)
+
+        prepare_x(1, 1)
+        turn_x(2, 0)
+        group_w(0, 1, nc.scalar.copy)
+        for t in range(PACK):
+            read_acc(0, t)
+        quantize_x(0, 0, BLOCK, CHUNK)
+        rectify(0, 0)
+        rectify(0, 1)
+        quantize_x(0, 1, BLOCK, CHUNK)
+        for t in range(PACK):
+            multiply(1, t)
+        rectify(0, 2)
+        rectify(0, 3)
+        group_w(1, 1, nc.scalar.copy, W_SPLIT2, P // 2)
+        group_x(2, 0)
+        prepare_x(3, 0)
+        prepare_x(2, 1)
+        for t in range(PACK):
+            read_acc(1, t)
+        group_w(1, 1, nc.vector.tensor_copy, 0, W_SPLIT2)
+        quantize_w(0, 1)
+        quantize_w(1, 1)
+        turn_x(3, 1)
+        multiply(2, 0)
+        group_x(3, 1)
+        for t in range(1, PACK):
+            multiply(2, t)
+        rectify_all(1)
+        group_y(1, nc.scalar.copy)
+        quantize_x(1, 0)
+        for t in range(PACK):
+            read_acc(2, t)
+        quantize_x(1, 1)
+        for t in range(PACK):
+            multiply(3, t)
+        rectify_all(2)
+        quantize_y(1)
+        turns = {3: [(4, 0), (5, 0)], 4: [(4, 1), (5, 1)], 5: [(6, 0), (7, 0)], 6: [(6, 1), (7, 1)]}
+        for s in range(3, last):
+            if s in (4, 6):
+                f = s // 2
+                for b, c in turns[s]:
+                    prepare_x(b, c)
+                group_y(s - 1, nc.scalar.copy)
+                quantize_x(f, 0)
+                for t in range(PACK):
+                    read_acc(s, t)
+                quantize_x(f, 1)
+                for t in range(PACK):
+                    multiply(s + 1, t)
+            else:
+                group_y(s - 1, nc.scalar.copy)
+                reads(s, turns.get(s, []))
+            rectify_all(s)
+            quantize_y(s - 1)
+        group_y(last - 1, nc.scalar.copy)
+        for t in range(3):
+            read_acc(last, t)
+        for t in range(2):
+            rectify(last, t)
+            store_y(last, t, t + 1)
+        read_acc(last, 3)
+        rectify(last, 2)
+        store_y(last, 2, 3)
+        quantize_y(last - 1)
+        rectify(last, 3)
+        store_y(last, 3, 4)
+        group_y(last, nc.vector.tensor_copy, 0, Y_SPLIT)
+        group_y(last, nc.scalar.copy, Y_SPLIT, CHUNK // 2)
+        quantize_y(last)
+        store_scales()

@@ -22,13 +22,12 @@ PASSES = CH // SPAN
 GROUPS = UNITS // SPAN
 CHUNK = 512
 BLOCK = 256
-STEPS = [(0, 0, 256), (0, 256, 256), (1, 0, 512), (0, 512, 512), (1, 512, 512),
-         (0, 1024, 512), (1, 1024, 512), (0, 1536, 512), (1, 1536, 512)]
-SHARED = [2, 3, 4, 5, 6, 7, 8]
+TILES = [(0, 0, 512), (1, 0, 512), (0, 512, 1024), (1, 512, 1024), (0, 1536, 512), (1, 1536, 512)]
+SHARED = [2, 3, 4, 5]
 W_SPLIT = 40
 W_SPLIT2 = 44
 Y_SPLIT = 160
-FINE = 5
+AHEAD = 5
 
 
 def tile_vocoder_prenet_units_first_g2_kernel(
@@ -38,8 +37,8 @@ def tile_vocoder_prenet_units_first_g2_kernel(
     with ExitStack() as ctx:
         keep = ctx.enter_context(tc.tile_pool(name="keep", bufs=1))
         stage = ctx.enter_context(tc.tile_pool(name="stage", bufs=2))
-        turn_psum = ctx.enter_context(tc.psum_pool(name="turn_psum", bufs=3))
-        acc_psum = ctx.enter_context(tc.psum_pool(name="acc_psum", bufs=5))
+        turn_psum = ctx.enter_context(tc.psum_pool(name="turn_psum", bufs=8 - AHEAD))
+        acc_psum = ctx.enter_context(tc.psum_pool(name="acc_psum", bufs=AHEAD))
         ctx.enter_context(tc.manual_schedule())
 
         w_raw, x_raw, masks_held = {}, {}, []
@@ -50,7 +49,7 @@ def tile_vocoder_prenet_units_first_g2_kernel(
             nc.sync.dma_start(out=w_raw[c, g][:], in_=rows.rearrange("(p j) u -> p j u", j=PACK))
 
         def load_x(b):
-            x_raw[b] = keep.tile([P, 2 * CH], BF16, name="x_raw_%d" % b)
+            x_raw[b] = stage.tile([P, 2 * CH], BF16, name="x_raw", bufs=6)
             rows = states[b * BLOCK : (b + 1) * BLOCK, :]
             nc.sync.dma_start(out=x_raw[b][:], in_=rows.rearrange("(r i) k -> r (i k)", i=2))
 
@@ -60,8 +59,7 @@ def tile_vocoder_prenet_units_first_g2_kernel(
             nc.sync.dma_start(out=held[:], in_=rows.rearrange("(p t) f -> p t f", t=PACK))
             masks_held.append((g, first, count, held))
 
-        def mask_of(s, t):
-            g, f0, n = STEPS[s]
+        def mask_of(g, t, f0, n):
             for group, first, count, held in masks_held:
                 if group == g and first <= f0 < first + count:
                     return held[:, t, f0 - first : f0 - first + n]
@@ -69,35 +67,12 @@ def tile_vocoder_prenet_units_first_g2_kernel(
 
         bias = keep.tile([P, GROUPS, PACK], BF16, name="bias")
         leak = keep.tile([P, GROUPS, PACK], BF16, name="leak")
-
-        load_w(0, 0)
-        load_x(0)
-        load_w(1, 0)
-        nc.sync.dma_start(out=bias[:], in_=prenet_b.rearrange("(g p t) -> p g t", p=P, t=PACK))
-        nc.sync.dma_start(out=leak[:], in_=slope.rearrange("(g p t) -> p g t", p=P, t=PACK))
-        load_x(1)
-        load_mask(0, 0, 512)
-        load_w(0, 1)
-        load_x(2)
-        load_w(1, 1)
-        load_x(3)
-        load_mask(1, 0, 512)
-        load_mask(0, 512, 512)
-        load_mask(1, 512, 512)
-        load_x(4)
-        load_x(5)
-        load_mask(0, 1024, 1024)
-        load_x(6)
-        load_x(7)
-        load_mask(1, 1024, 1024)
-
         ident = keep.tile([P, P], F32, name="ident")
-        make_identity(nc, ident[:])
+        y_scales = keep.tile([P, FRAMES], U8, name="y_scales", align_bytes=64)
 
         w_grouped, w_codes, w_scales = {}, {}, {}
         x_grouped, x_codes, x_scales = {}, {}, {}
-        acc, y, y_grouped, low, whole = {}, {}, {}, {}, {}
-        y_scales = keep.tile([P, FRAMES], U8, name="y_scales", align_bytes=64)
+        turned, acc, y, y_grouped, low = {}, {}, {}, {}, {}
 
         def group_w(c, g, copy, lo=0, hi=P // 2):
             if (c, g) not in w_grouped:
@@ -114,8 +89,6 @@ def tile_vocoder_prenet_units_first_g2_kernel(
                 out=w_codes[c, g][:].bitcast(FP8X4), scales=w_scales[c, g][:], in_=w_grouped[c, g][:]
             )
 
-        turned = {}
-
         def turn_x(b, c):
             turned[b, c] = turn_psum.tile([P, 4, P], F32, name="turned")
             words = x_raw[b][:].bitcast(F32)
@@ -128,9 +101,10 @@ def tile_vocoder_prenet_units_first_g2_kernel(
 
         def group_x(b, c):
             f, half = divmod(b, 2)
-            if half == 0:
-                x_grouped[f, c] = stage.tile([P, PACK * CHUNK], BF16, name="x_grouped", bufs=3, align_bytes=64)
-            words = x_grouped[f, c][:].bitcast(F32)[:, half * 2 * BLOCK : (half + 1) * 2 * BLOCK]
+            if f not in x_grouped:
+                x_grouped[f] = stage.tile([P, PASSES * PACK * CHUNK], BF16, name="x_grouped", align_bytes=64)
+            first = 2 * (c * CHUNK + half * BLOCK)
+            words = x_grouped[f][:].bitcast(F32)[:, first : first + 2 * BLOCK]
             nc.scalar.copy(
                 out=words.rearrange("p (r q) -> p r q", q=4), in_=turned[b, c][:].rearrange("p q r -> p r q")
             )
@@ -139,87 +113,93 @@ def tile_vocoder_prenet_units_first_g2_kernel(
             turn_x(b, c)
             group_x(b, c)
 
-        def quantize_x(f, c, lo=0, hi=CHUNK):
-            if (f, c) not in x_codes:
-                x_codes[f, c] = keep.tile([P, CHUNK], U32, name="x_codes_%d_%d" % (f, c), align_bytes=64)
-                x_scales[f, c] = keep.tile([P, CHUNK], U8, name="x_scales_%d_%d" % (f, c), align_bytes=64)
+        def quantize_x(f, lo=0, hi=PASSES * CHUNK):
+            if f not in x_codes:
+                x_codes[f] = keep.tile([P, PASSES * CHUNK], U32, name="x_codes_%d" % f, align_bytes=64)
+                x_scales[f] = keep.tile([P, PASSES * CHUNK], U8, name="x_scales_%d" % f, align_bytes=64)
             nc.vector.quantize_mx(
-                out=x_codes[f, c][:, lo:hi].bitcast(FP8X4), scales=x_scales[f, c][:, lo:hi],
-                in_=x_grouped[f, c][:, PACK * lo : PACK * hi],
+                out=x_codes[f][:, lo:hi].bitcast(FP8X4), scales=x_scales[f][:, lo:hi],
+                in_=x_grouped[f][:, PACK * lo : PACK * hi],
             )
 
-        def multiply(s, t):
-            g, f0, n = STEPS[s]
-            f, lo = divmod(f0, CHUNK)
-            acc[s, t] = acc_psum.tile([P, n], F32, name="acc")
+        def multiply(k, t, lo, n, passes=range(PASSES)):
+            g, f0, width = TILES[k]
+            f, first = divmod(f0 + lo, CHUNK)
+            if (k, t, lo) not in acc:
+                acc[k, t, lo] = acc_psum.tile([P, n], F32, name="acc")
             cols = slice(t * P, (t + 1) * P)
-            for c in range(PASSES):
+            for c in passes:
+                frames = slice(c * CHUNK + first, c * CHUNK + first + n)
                 nc.tensor.matmul_mx(
-                    out=acc[s, t][:],
+                    out=acc[k, t, lo][:],
                     lhsT=w_codes[c, g][:, cols].bitcast(FP8X4),
                     lhsT_scale=w_scales[c, g][:, cols],
-                    rhs=x_codes[f, c][:, lo : lo + n].bitcast(FP8X4),
-                    rhs_scale=x_scales[f, c][:, lo : lo + n],
+                    rhs=x_codes[f][:, frames].bitcast(FP8X4),
+                    rhs_scale=x_scales[f][:, frames],
                     start=(c == 0),
                     stop=(c == PASSES - 1),
                 )
-            if t == 0 and s in SHARED:
-                low[s] = stage.tile([P, CHUNK], F32, name="low")
-                nc.scalar.activation(
-                    out=low[s][:, :n], in_=acc[s, t][:], func=ACT.Identity,
-                    scale=leak_f32[:, g : g + 1], bias=leak_bias[:, g : g + 1],
-                )
 
-        def read_acc(s, t):
-            g, f0, n = STEPS[s]
-            if t == 0 and s != 1:
-                whole[s] = keep.tile([P, PACK, CHUNK], F32, name="y_%d" % s)
-                y[s] = whole[s][:, :, :n]
-            if t == 0 and s == 1:
-                whole[1] = whole[0]
-                y[1] = whole[1][:, :, BLOCK:]
-            if t == 0 and s in SHARED:
+        def slope_side(k, lo, n):
+            g = TILES[k][0]
+            low[k, lo] = stage.tile([P, CHUNK], F32, name="low", bufs=4)
+            nc.scalar.activation(
+                out=low[k, lo][:, :n], in_=acc[k, 0, lo][:], func=ACT.Identity,
+                scale=leak_f32[:, g : g + 1], bias=leak_bias[:, g : g + 1],
+            )
+
+        def read_acc(k, t, lo, n):
+            g, f0, width = TILES[k]
+            if k not in y:
+                y[k] = keep.tile([P, PACK, width], F32, name="y_%d" % k)
+            mask = mask_of(g, t, f0 + lo, n)
+            if t == 0 and k in SHARED:
                 nc.vector.scalar_tensor_tensor(
-                    out=low[s][:, :n], in0=acc[s, t][:], scalar=bias[:, g, t : t + 1], in1=low[s][:, :n],
+                    out=low[k, lo][:, :n], in0=acc[k, t, lo][:], scalar=bias[:, g, t : t + 1], in1=low[k, lo][:, :n],
                     op0=ALU.add, op1=ALU.max,
                 )
-                nc.gpsimd.tensor_tensor(out=y[s][:, t, :], in0=low[s][:, :n], in1=mask_of(s, t), op=ALU.mult)
+                nc.gpsimd.tensor_tensor(out=y[k][:, t, lo : lo + n], in0=low[k, lo][:, :n], in1=mask, op=ALU.mult)
             else:
                 nc.vector.scalar_tensor_tensor(
-                    out=y[s][:, t, :], in0=acc[s, t][:], scalar=bias[:, g, t : t + 1], in1=mask_of(s, t),
+                    out=y[k][:, t, lo : lo + n], in0=acc[k, t, lo][:], scalar=bias[:, g, t : t + 1], in1=mask,
                     op0=ALU.add, op1=ALU.mult,
                 )
 
-        def rectify(s, t):
-            g, f0, n = STEPS[s]
-            if not (t == 0 and s in SHARED):
+        def rectify(k, t, lo=0, n=None):
+            g, f0, width = TILES[k]
+            part = y[k][:, t, lo : lo + (n or width)]
+            if not (t == 0 and k in SHARED):
                 nc.vector.scalar_tensor_tensor(
-                    out=y[s][:, t, :], in0=y[s][:, t, :], scalar=leak[:, g, t : t + 1], in1=y[s][:, t, :],
-                    op0=ALU.mult, op1=ALU.max,
+                    out=part, in0=part, scalar=leak[:, g, t : t + 1], in1=part, op0=ALU.mult, op1=ALU.max
                 )
 
-        def store_y(s, lo=0, hi=PACK):
-            g, f0, n = STEPS[s]
-            f0 = f0 // CHUNK * CHUNK
-            rows = out_0[g * SPAN : (g + 1) * SPAN, f0 : f0 + CHUNK]
-            nc.sync.dma_start(out=rows.rearrange("(p t) f -> p t f", t=PACK)[:, lo:hi, :], in_=whole[s][:, lo:hi, :])
+        def store_y(k, lo=0, hi=PACK):
+            g, f0, width = TILES[k]
+            rows = out_0[g * SPAN : (g + 1) * SPAN, f0 : f0 + width]
+            nc.sync.dma_start(out=rows.rearrange("(p t) f -> p t f", t=PACK)[:, lo:hi, :], in_=y[k][:, lo:hi, :])
 
-        def group_y(s, copy, lo=0, hi=CHUNK // 2):
-            if s not in y_grouped:
-                y_grouped[s] = stage.tile([P, PACK * CHUNK], BF16, name="y_grouped", align_bytes=64)
+        def group_y(k, copy, lo=0, hi=None):
+            width = TILES[k][2]
+            if k not in y_grouped:
+                y_grouped[k] = stage.tile([P, PACK * width], BF16, name="y_grouped", align_bytes=64)
+            hi = hi or width // 2
             copy(
-                out=y_grouped[s][:].rearrange("p (c i t) -> p c t i", i=2, t=PACK)[:, lo:hi],
-                in_=whole[s][:].rearrange("p t (c i) -> p c t i", i=2)[:, lo:hi],
+                out=y_grouped[k][:].rearrange("p (f t) -> p f t", t=PACK)[:, 2 * lo : 2 * hi],
+                in_=y[k][:].rearrange("p t f -> p f t")[:, 2 * lo : 2 * hi],
             )
 
-        def quantize_y(s):
-            g, f0, n = STEPS[s]
-            f0 = f0 // CHUNK * CHUNK
-            cols = slice(f0, f0 + CHUNK)
-            y_codes = keep.tile([P, CHUNK], U32, name="y_codes_%d" % s, align_bytes=64)
-            nc.vector.quantize_mx(out=y_codes[:].bitcast(FP8X4), scales=y_scales[4 * g :, cols], in_=y_grouped[s][:])
+        def quantize_y(k):
+            g, f0, width = TILES[k]
+            y_codes = keep.tile([P, width], U32, name="y_codes_%d" % k, align_bytes=64)
+            for lo in range(0, width, CHUNK):
+                nc.vector.quantize_mx(
+                    out=y_codes[:, lo : lo + CHUNK].bitcast(FP8X4),
+                    scales=y_scales[4 * g :, f0 + lo : f0 + lo + CHUNK],
+                    in_=y_grouped[k][:, PACK * lo : PACK * (lo + CHUNK)],
+                )
             nc.sync.dma_start(
-                out=out_1[g, :, cols, :].rearrange("p m t -> p (m t)").bitcast(I32), in_=y_codes[:].bitcast(I32)
+                out=out_1[g, :, f0 : f0 + width, :].rearrange("p m t -> p (m t)").bitcast(I32),
+                in_=y_codes[:].bitcast(I32),
             )
 
         def store_scales():
@@ -230,115 +210,164 @@ def tile_vocoder_prenet_units_first_g2_kernel(
                     in_=y_scales[32 * q : 32 * q + 4 * GROUPS, :].bitcast(I32),
                 )
 
+        banks = [(0, t, 0, BLOCK) for t in range(PACK)] + [(0, t, BLOCK, BLOCK) for t in range(PACK)]
+        for k in range(1, 4):
+            banks.extend([(k, t, lo, CHUNK) for t in range(PACK) for lo in range(0, TILES[k][2], CHUNK)])
+        banks.extend([(4, 0, 0, CHUNK), (5, 0, 0, CHUNK)])
+        banks.extend([(k, t, 0, CHUNK) for k in (4, 5) for t in range(1, PACK)])
+        cursor = {"filled": 0, "read": 0}
+
+        def fill(upto):
+            for i in range(cursor["filled"], min(len(banks), cursor["read"] + AHEAD)):
+                if (banks[i][0], banks[i][2] if banks[i][0] == 0 else 0) > upto:
+                    break
+                multiply(*banks[i])
+                cursor["filled"] = i + 1
+
+        def fill_pass(c):
+            for i in range(cursor["filled"], cursor["filled"] + PACK):
+                multiply(*banks[i], passes=[c])
+            if c == PASSES - 1:
+                cursor["filled"] = cursor["filled"] + PACK
+
+        def empty(count, upto, between=()):
+            for i in range(count):
+                read_acc(*banks[cursor["read"]])
+                cursor["read"] = cursor["read"] + 1
+                fill(upto)
+                if i < len(between):
+                    prepare_x(*between[i])
+
+        def slope_sides(k):
+            if k in SHARED:
+                for lo in range(0, TILES[k][2], CHUNK):
+                    slope_side(k, lo, CHUNK)
+
+        load_w(0, 0)
+        load_x(0)
+        load_w(1, 0)
+        nc.sync.dma_start(out=bias[:], in_=prenet_b.rearrange("(g p t) -> p g t", p=P, t=PACK))
+        nc.sync.dma_start(out=leak[:], in_=slope.rearrange("(g p t) -> p g t", p=P, t=PACK))
+        load_x(1)
+        load_mask(0, 0, 512)
+        load_w(0, 1)
+        load_x(2)
+        load_w(1, 1)
+        load_x(3)
+        load_mask(1, 0, 512)
+        load_x(4)
+        load_x(5)
+        load_mask(0, 512, 1536)
+        load_mask(1, 512, 1536)
+
+        make_identity(nc, ident[:])
         if SHARED:
             warm = keep.tile([P, 1], F32, name="warm")
             nc.scalar.activation(out=warm[:], in_=ident[:, 0:1], func=ACT.Identity)
+
         group_w(0, 0, nc.vector.tensor_copy)
         quantize_w(0, 0)
         prepare_x(0, 0)
         group_w(1, 0, nc.vector.tensor_copy, 0, W_SPLIT)
         group_w(1, 0, nc.scalar.copy, W_SPLIT, P // 2)
         prepare_x(0, 1)
-        quantize_x(0, 0, 0, BLOCK)
+        quantize_x(0, 0, BLOCK)
         quantize_w(1, 0)
-        quantize_x(0, 1, 0, BLOCK)
+        quantize_x(0, CHUNK, CHUNK + BLOCK)
         if SHARED:
             leak_f32 = keep.tile([P, GROUPS], F32, name="leak_f32")
             leak_bias = keep.tile([P, GROUPS], F32, name="leak_bias")
-            nc.gpsimd.tensor_copy(out=leak_f32[:], in_=leak[:, :, 0])
-            nc.gpsimd.tensor_tensor(out=leak_bias[:], in0=leak[:, :, 0], in1=bias[:, :, 0], op=ALU.mult)
+            nc.vector.tensor_copy(out=leak_f32[:], in_=leak[:, :, 0])
+            nc.vector.tensor_tensor(out=leak_bias[:], in0=leak[:, :, 0], in1=bias[:, :, 0], op=ALU.mult)
         prepare_x(1, 0)
-        for t in range(PACK):
-            multiply(0, t)
-        last = len(STEPS) - 1
-
-        def reads(s, between):
-            multiply(s + 1, 0)
-            for t in range(PACK):
-                read_acc(s, t)
-                if t < len(between):
-                    prepare_x(*between[t])
-                if t + 1 < PACK:
-                    multiply(s + 1, t + 1)
-
-        def rectify_all(s):
-            if s >= FINE and s in SHARED:
-                store_y(s, 0, 1)
-            for t in range(PACK):
-                rectify(s, t)
-                if s >= FINE and not (t == 0 and s in SHARED):
-                    store_y(s, t, t + 1)
-            if s < FINE:
-                store_y(s)
-
+        fill((0, 0))
         prepare_x(1, 1)
+        load_x(6)
+        load_x(7)
         turn_x(2, 0)
         group_w(0, 1, nc.scalar.copy)
-        for t in range(PACK):
-            read_acc(0, t)
-        quantize_x(0, 0, BLOCK, CHUNK)
-        rectify(0, 0)
-        rectify(0, 1)
-        quantize_x(0, 1, BLOCK, CHUNK)
-        for t in range(PACK):
-            multiply(1, t)
-        rectify(0, 2)
-        rectify(0, 3)
+        empty(4, (0, 0))
+        quantize_x(0, BLOCK, CHUNK)
+        rectify(0, 0, 0, BLOCK)
+        rectify(0, 1, 0, BLOCK)
+        quantize_x(0, CHUNK + BLOCK, 2 * CHUNK)
+        fill((0, BLOCK))
+        rectify(0, 2, 0, BLOCK)
+        rectify(0, 3, 0, BLOCK)
+
         group_w(1, 1, nc.scalar.copy, W_SPLIT2, P // 2)
         group_x(2, 0)
         prepare_x(3, 0)
         prepare_x(2, 1)
-        for t in range(PACK):
-            read_acc(1, t)
-        group_w(1, 1, nc.vector.tensor_copy, 0, W_SPLIT2)
+        empty(4, (0, BLOCK))
+        rectify(0, 0, BLOCK, BLOCK)
         quantize_w(0, 1)
+        fill_pass(0)
+        group_w(1, 1, nc.vector.tensor_copy, 0, W_SPLIT2)
+        rectify(0, 1, BLOCK, BLOCK)
+        prepare_x(3, 1)
         quantize_w(1, 1)
-        turn_x(3, 1)
-        multiply(2, 0)
-        group_x(3, 1)
-        for t in range(1, PACK):
-            multiply(2, t)
-        rectify_all(1)
+        fill_pass(1)
+        slope_sides(1)
+        for t in range(2, PACK):
+            rectify(0, t, BLOCK, BLOCK)
+        store_y(0)
+        group_y(0, nc.scalar.copy, 0, CHUNK // 4)
+
+        prepare_x(4, 0)
+        prepare_x(5, 0)
+        prepare_x(4, 1)
+        prepare_x(5, 1)
+        empty(4, (1, 0))
+        quantize_x(1)
+        rectify(1, 0)
+        rectify(1, 1)
+        quantize_x(2)
+        fill((2, 0))
+        slope_sides(2)
+        group_y(0, nc.scalar.copy, CHUNK // 4, CHUNK // 2)
+        rectify(1, 2)
+        rectify(1, 3)
+        store_y(1)
         group_y(1, nc.scalar.copy)
-        quantize_x(1, 0)
+
+        empty(8, (3, 0))
+        slope_sides(3)
+        for b, c in [(6, 0), (7, 0), (6, 1), (7, 1)]:
+            prepare_x(b, c)
+        quantize_y(0)
         for t in range(PACK):
-            read_acc(2, t)
-        quantize_x(1, 1)
+            rectify(2, t)
+            if t % 2 == 1:
+                store_y(2, t - 1, t + 1)
+            if t == 1:
+                quantize_y(1)
+        group_y(2, nc.scalar.copy)
+        quantize_x(3)
+
+        empty(8, (5, 0))
+        slope_sides(4)
+        slope_sides(5)
         for t in range(PACK):
-            multiply(3, t)
-        rectify_all(2)
-        quantize_y(1)
-        turns = {3: [(4, 0), (5, 0)], 4: [(4, 1), (5, 1)], 5: [(6, 0), (7, 0)], 6: [(6, 1), (7, 1)]}
-        for s in range(3, last):
-            if s in (4, 6):
-                f = s // 2
-                for b, c in turns[s]:
-                    prepare_x(b, c)
-                group_y(s - 1, nc.scalar.copy)
-                quantize_x(f, 0)
-                for t in range(PACK):
-                    read_acc(s, t)
-                quantize_x(f, 1)
-                for t in range(PACK):
-                    multiply(s + 1, t)
-            else:
-                group_y(s - 1, nc.scalar.copy)
-                reads(s, turns.get(s, []))
-            rectify_all(s)
-            quantize_y(s - 1)
-        group_y(last - 1, nc.scalar.copy)
-        for t in range(3):
-            read_acc(last, t)
-        for t in range(2):
-            rectify(last, t)
-            store_y(last, t, t + 1)
-        read_acc(last, 3)
-        rectify(last, 2)
-        store_y(last, 2, 3)
-        quantize_y(last - 1)
-        rectify(last, 3)
-        store_y(last, 3, 4)
-        group_y(last, nc.vector.tensor_copy, 0, Y_SPLIT)
-        group_y(last, nc.scalar.copy, Y_SPLIT, CHUNK // 2)
-        quantize_y(last)
+            rectify(3, t)
+            store_y(3, t, t + 1)
+        quantize_y(2)
+        group_y(3, nc.scalar.copy)
+
+        empty(6, (5, 0))
+        store_y(4, 0, 1)
+        store_y(5, 0, 1)
+        for t in range(1, PACK):
+            rectify(4, t)
+            store_y(4, t, t + 1)
+        group_y(4, nc.scalar.copy)
+        quantize_y(3)
+        empty(2, (5, 0))
+        for t in range(1, PACK):
+            rectify(5, t)
+            store_y(5, t, t + 1)
+        quantize_y(4)
+        group_y(5, nc.vector.tensor_copy, 0, Y_SPLIT)
+        group_y(5, nc.scalar.copy, Y_SPLIT, CHUNK // 2)
+        quantize_y(5)
         store_scales()

@@ -13,7 +13,7 @@ U32 = mybir.dt.uint32
 U8 = mybir.dt.uint8
 FP8X4 = mybir.dt.float8_e4m3fn_x4
 ALU = mybir.AluOpType
-ACT = mybir.ActivationFunctionType
+IDENTITY = mybir.ActivationFunctionType.Identity
 
 P = 128
 PACK = 4
@@ -22,12 +22,26 @@ PASSES = CH // SPAN
 GROUPS = UNITS // SPAN
 CHUNK = 512
 BLOCK = 256
-TILES = [(0, 0, 512), (1, 0, 512), (0, 512, 1024), (1, 512, 1024), (0, 1536, 512), (1, 1536, 512)]
-SHARED = [2, 3, 4, 5]
-W_SPLIT = 40
-W_SPLIT2 = 44
-Y_SPLIT = 160
-AHEAD = 5
+QUADRANT = 32
+SCALE_ROWS = 4
+
+TILES = [(0, 0, CHUNK), (1, 0, CHUNK), (0, CHUNK, 2 * CHUNK), (1, CHUNK, 2 * CHUNK),
+         (0, 3 * CHUNK, CHUNK), (1, 3 * CHUNK, CHUNK)]
+LAST_CHUNK = FRAMES - CHUNK
+
+PRODUCTS = [(0, t, lo, BLOCK) for lo in (0, BLOCK) for t in range(PACK)] + [
+    (k, t, lo, CHUNK) for k in range(1, len(TILES)) for lo in range(0, TILES[k][2], CHUNK) for t in range(PACK)
+]
+RUN = 8
+GPSIMD_SLOTS = 3
+VIA_GPSIMD = [(k, t, 0) for k in (2, 3, 4) for t in range(GPSIMD_SLOTS)]
+
+BANKS = 8
+TURN_BANKS = 3
+
+HEAD_W_SLOTS = 3
+NEXT_W_SLOTS = 2
+TAIL_FRAMES = 320
 
 
 def tile_vocoder_prenet_units_first_g2_kernel(
@@ -37,11 +51,15 @@ def tile_vocoder_prenet_units_first_g2_kernel(
     with ExitStack() as ctx:
         keep = ctx.enter_context(tc.tile_pool(name="keep", bufs=1))
         stage = ctx.enter_context(tc.tile_pool(name="stage", bufs=2))
-        turn_psum = ctx.enter_context(tc.psum_pool(name="turn_psum", bufs=8 - AHEAD))
-        acc_psum = ctx.enter_context(tc.psum_pool(name="acc_psum", bufs=AHEAD))
+        psum = ctx.enter_context(tc.psum_pool(name="psum", bufs=1))
         ctx.enter_context(tc.manual_schedule())
 
-        w_raw, x_raw, masks_held = {}, {}, []
+        w_raw, w_sorted, w_codes, w_scales = {}, {}, {}, {}
+        x_raw, x_turned, x_sorted, x_codes, x_scales = {}, {}, {}, {}, {}
+        mask, sums, bank_of, sloped, y, y_sorted = {}, {}, {}, {}, {}, {}
+        free_banks = list(range(TURN_BANKS, BANKS))
+        count = {"made": 0, "read": 0}
+
 
         def load_w(c, g):
             w_raw[c, g] = keep.tile([P, PACK, SPAN], BF16, name="w_raw_%d_%d" % (c, g))
@@ -53,321 +71,310 @@ def tile_vocoder_prenet_units_first_g2_kernel(
             rows = states[b * BLOCK : (b + 1) * BLOCK, :]
             nc.sync.dma_start(out=x_raw[b][:], in_=rows.rearrange("(r i) k -> r (i k)", i=2))
 
-        def load_mask(g, first, count):
-            held = keep.tile([P, PACK, count], BF16, name="mask_%d_%d" % (g, first))
-            rows = drop_mask[g * SPAN : (g + 1) * SPAN, first : first + count]
+        def load_mask(g, first, frames):
+            held = keep.tile([P, PACK, frames], BF16, name="mask_%d_%d" % (g, first))
+            rows = drop_mask[g * SPAN : (g + 1) * SPAN, first : first + frames]
             nc.sync.dma_start(out=held[:], in_=rows.rearrange("(p t) f -> p t f", t=PACK))
-            masks_held.append((g, first, count, held))
+            for lo in range(0, frames, CHUNK):
+                mask[g, first + lo] = held[:, :, lo : lo + CHUNK]
 
-        def mask_of(g, t, f0, n):
-            for group, first, count, held in masks_held:
-                if group == g and first <= f0 < first + count:
-                    return held[:, t, f0 - first : f0 - first + n]
-            raise ValueError("no mask tile")
 
-        bias = keep.tile([P, GROUPS, PACK], BF16, name="bias")
-        leak = keep.tile([P, GROUPS, PACK], BF16, name="leak")
-        ident = keep.tile([P, P], F32, name="ident")
-        y_scales = keep.tile([P, FRAMES], U8, name="y_scales", align_bytes=64)
-
-        w_grouped, w_codes, w_scales = {}, {}, {}
-        x_grouped, x_codes, x_scales = {}, {}, {}
-        turned, acc, y, y_grouped, low = {}, {}, {}, {}, {}
-
-        def group_w(c, g, copy, lo=0, hi=P // 2):
-            if (c, g) not in w_grouped:
-                w_grouped[c, g] = stage.tile([P, PACK * SPAN], BF16, name="w_grouped", align_bytes=64)
+        def sort_w(c, g, copy, first=0, last=PACK):
+            if (c, g) not in w_sorted:
+                w_sorted[c, g] = stage.tile([P, PACK * SPAN], BF16, name="w_sorted", align_bytes=64)
             copy(
-                out=w_grouped[c, g][:].rearrange("p (t m n j) -> p m t n j", t=PACK, n=2, j=PACK)[:, lo:hi],
-                in_=w_raw[c, g][:].rearrange("p j (m n t) -> p m t n j", n=2, t=PACK)[:, lo:hi],
+                out=w_sorted[c, g][:].rearrange("p (t h n j) -> p h t n j", t=PACK, n=2, j=PACK)[:, :, first:last],
+                in_=w_raw[c, g][:].rearrange("p j (h n t) -> p h t n j", n=2, t=PACK)[:, :, first:last],
             )
 
         def quantize_w(c, g):
             w_codes[c, g] = keep.tile([P, SPAN], U32, name="w_codes_%d_%d" % (c, g), align_bytes=64)
             w_scales[c, g] = keep.tile([P, SPAN], U8, name="w_scales_%d_%d" % (c, g), align_bytes=64)
             nc.vector.quantize_mx(
-                out=w_codes[c, g][:].bitcast(FP8X4), scales=w_scales[c, g][:], in_=w_grouped[c, g][:]
+                out=w_codes[c, g][:].bitcast(FP8X4), scales=w_scales[c, g][:], in_=w_sorted[c, g][:]
             )
+
 
         def turn_x(b, c):
-            turned[b, c] = turn_psum.tile([P, 4, P], F32, name="turned")
-            words = x_raw[b][:].bitcast(F32)
+            bank = len(x_turned) % TURN_BANKS
+            x_turned[b, c] = psum.tile([P, 4, P], F32, name="x_turned", tag="bank_%d" % bank)
+            pairs = x_raw[b][:].bitcast(F32)
             for i in range(2):
+                first = i * (CH // 2) + c * (SPAN // 2)
                 for u in range(2):
-                    first = i * (CH // 2) + c * (SPAN // 2)
                     nc.tensor.transpose(
-                        turned[b, c][:, 2 * i + u, :], words[:, first + u : first + SPAN // 2 : 2], ident[:]
+                        x_turned[b, c][:, 2 * i + u, :], pairs[:, first + u : first + SPAN // 2 : 2], ident[:]
                     )
 
-        def group_x(b, c):
-            f, half = divmod(b, 2)
-            if f not in x_grouped:
-                x_grouped[f] = stage.tile([P, PASSES * PACK * CHUNK], BF16, name="x_grouped", align_bytes=64)
+        def sort_x(b, c):
+            chunk, half = divmod(b, 2)
+            if chunk not in x_sorted:
+                x_sorted[chunk] = stage.tile([P, PASSES * PACK * CHUNK], BF16, name="x_sorted", align_bytes=64)
             first = 2 * (c * CHUNK + half * BLOCK)
-            words = x_grouped[f][:].bitcast(F32)[:, first : first + 2 * BLOCK]
+            pairs = x_sorted[chunk][:].bitcast(F32)[:, first : first + 2 * BLOCK]
             nc.scalar.copy(
-                out=words.rearrange("p (r q) -> p r q", q=4), in_=turned[b, c][:].rearrange("p q r -> p r q")
+                out=pairs.rearrange("p (r q) -> p r q", q=4), in_=x_turned[b, c][:].rearrange("p q r -> p r q")
             )
 
-        def prepare_x(b, c):
+        def turn_and_sort_x(b, c):
             turn_x(b, c)
-            group_x(b, c)
+            sort_x(b, c)
 
-        def quantize_x(f, lo=0, hi=PASSES * CHUNK):
-            if f not in x_codes:
-                x_codes[f] = keep.tile([P, PASSES * CHUNK], U32, name="x_codes_%d" % f, align_bytes=64)
-                x_scales[f] = keep.tile([P, PASSES * CHUNK], U8, name="x_scales_%d" % f, align_bytes=64)
+        def turn_and_sort_chunk(chunk):
+            for c in range(PASSES):
+                for b in (2 * chunk, 2 * chunk + 1):
+                    turn_and_sort_x(b, c)
+
+        def quantize_x(chunk, first=0, words=PASSES * CHUNK):
+            if chunk not in x_codes:
+                x_codes[chunk] = keep.tile([P, PASSES * CHUNK], U32, name="x_codes_%d" % chunk, align_bytes=64)
+                x_scales[chunk] = keep.tile([P, PASSES * CHUNK], U8, name="x_scales_%d" % chunk, align_bytes=64)
             nc.vector.quantize_mx(
-                out=x_codes[f][:, lo:hi].bitcast(FP8X4), scales=x_scales[f][:, lo:hi],
-                in_=x_grouped[f][:, PACK * lo : PACK * hi],
+                out=x_codes[chunk][:, first : first + words].bitcast(FP8X4),
+                scales=x_scales[chunk][:, first : first + words],
+                in_=x_sorted[chunk][:, PACK * first : PACK * (first + words)],
             )
 
-        def multiply(k, t, lo, n, passes=range(PASSES)):
-            g, f0, width = TILES[k]
-            f, first = divmod(f0 + lo, CHUNK)
-            if (k, t, lo) not in acc:
-                acc[k, t, lo] = acc_psum.tile([P, n], F32, name="acc")
-            cols = slice(t * P, (t + 1) * P)
-            for c in passes:
-                frames = slice(c * CHUNK + first, c * CHUNK + first + n)
-                nc.tensor.matmul_mx(
-                    out=acc[k, t, lo][:],
-                    lhsT=w_codes[c, g][:, cols].bitcast(FP8X4),
-                    lhsT_scale=w_scales[c, g][:, cols],
-                    rhs=x_codes[f][:, frames].bitcast(FP8X4),
-                    rhs_scale=x_scales[f][:, frames],
-                    start=(c == 0),
-                    stop=(c == PASSES - 1),
+        def quantize_block(b, c):
+            quantize_x(b // 2, c * CHUNK + (b % 2) * BLOCK, BLOCK)
+
+
+        def multiply(k, t, lo, frames, c):
+            g, first, width = TILES[k]
+            chunk, start = divmod(first + lo, CHUNK)
+            if c == 0:
+                bank_of[k, t, lo] = free_banks.pop(0)
+                sums[k, t, lo] = psum.tile([P, frames], F32, name="sums", tag="bank_%d" % bank_of[k, t, lo])
+            units = slice(t * P, (t + 1) * P)
+            words = slice(c * CHUNK + start, c * CHUNK + start + frames)
+            nc.tensor.matmul_mx(
+                out=sums[k, t, lo][:],
+                lhsT=w_codes[c, g][:, units].bitcast(FP8X4),
+                lhsT_scale=w_scales[c, g][:, units],
+                rhs=x_codes[chunk][:, words].bitcast(FP8X4),
+                rhs_scale=x_scales[chunk][:, words],
+                start=(c == 0),
+                stop=(c == PASSES - 1),
+            )
+
+        def products_before(k, lo=0):
+            return PRODUCTS.index((k, 0, lo, BLOCK if k == 0 else CHUNK))
+
+        def make_products(ready):
+            for i in range(count["made"], min(ready, count["made"] + len(free_banks))):
+                for c in range(PASSES):
+                    multiply(*PRODUCTS[i], c)
+                count["made"] = i + 1
+
+        def apply_slope(k):
+            g = TILES[k][0]
+            for t in range(GPSIMD_SLOTS):
+                sloped[k, t] = stage.tile([P, CHUNK], F32, name="sloped", bufs=GPSIMD_SLOTS + 1)
+                nc.scalar.activation(
+                    out=sloped[k, t][:], in_=sums[k, t, 0][:], func=IDENTITY,
+                    scale=slope_f32[:, g, t : t + 1], bias=slope_bias[:, g, t : t + 1],
                 )
 
-        def slope_side(k, lo, n):
-            g = TILES[k][0]
-            low[k, lo] = stage.tile([P, CHUNK], F32, name="low", bufs=4)
-            nc.scalar.activation(
-                out=low[k, lo][:, :n], in_=acc[k, 0, lo][:], func=ACT.Identity,
-                scale=leak_f32[:, g : g + 1], bias=leak_bias[:, g : g + 1],
-            )
-
-        def read_acc(k, t, lo, n):
-            g, f0, width = TILES[k]
+        def read_product(k, t, lo, frames):
+            g, first, width = TILES[k]
             if k not in y:
                 y[k] = keep.tile([P, PACK, width], F32, name="y_%d" % k)
-            mask = mask_of(g, t, f0 + lo, n)
-            if t == 0 and k in SHARED:
+            start = (first + lo) % CHUNK
+            kept = mask[g, first + lo - start][:, t, start : start + frames]
+            part = y[k][:, t, lo : lo + frames]
+            if (k, t, lo) in VIA_GPSIMD:
                 nc.vector.scalar_tensor_tensor(
-                    out=low[k, lo][:, :n], in0=acc[k, t, lo][:], scalar=bias[:, g, t : t + 1], in1=low[k, lo][:, :n],
+                    out=sloped[k, t][:], in0=sums[k, t, lo][:], scalar=bias[:, g, t : t + 1], in1=sloped[k, t][:],
                     op0=ALU.add, op1=ALU.max,
                 )
-                nc.gpsimd.tensor_tensor(out=y[k][:, t, lo : lo + n], in0=low[k, lo][:, :n], in1=mask, op=ALU.mult)
+                nc.gpsimd.tensor_tensor(out=part, in0=sloped[k, t][:], in1=kept, op=ALU.mult)
             else:
                 nc.vector.scalar_tensor_tensor(
-                    out=y[k][:, t, lo : lo + n], in0=acc[k, t, lo][:], scalar=bias[:, g, t : t + 1], in1=mask,
+                    out=part, in0=sums[k, t, lo][:], scalar=bias[:, g, t : t + 1], in1=kept,
                     op0=ALU.add, op1=ALU.mult,
                 )
+            free_banks.append(bank_of[k, t, lo])
 
-        def rectify(k, t, lo=0, n=None):
-            g, f0, width = TILES[k]
-            part = y[k][:, t, lo : lo + (n or width)]
-            if not (t == 0 and k in SHARED):
-                nc.vector.scalar_tensor_tensor(
-                    out=part, in0=part, scalar=leak[:, g, t : t + 1], in1=part, op0=ALU.mult, op1=ALU.max
-                )
+        def read_products(n, ready):
+            for i in range(count["read"], count["read"] + n):
+                read_product(*PRODUCTS[i])
+                make_products(ready)
+            count["read"] = count["read"] + n
 
-        def store_y(k, lo=0, hi=PACK):
-            g, f0, width = TILES[k]
-            rows = out_0[g * SPAN : (g + 1) * SPAN, f0 : f0 + width]
-            nc.sync.dma_start(out=rows.rearrange("(p t) f -> p t f", t=PACK)[:, lo:hi, :], in_=y[k][:, lo:hi, :])
+        def rectify(k, t, lo, hi):
+            part = y[k][:, t, lo:hi]
+            nc.vector.scalar_tensor_tensor(
+                out=part, in0=part, scalar=slope_bf16[:, TILES[k][0], t : t + 1], in1=part, op0=ALU.mult, op1=ALU.max
+            )
 
-        def group_y(k, copy, lo=0, hi=None):
-            width = TILES[k][2]
-            if k not in y_grouped:
-                y_grouped[k] = stage.tile([P, PACK * width], BF16, name="y_grouped", align_bytes=64)
-            hi = hi or width // 2
+        def rectify_rest(k, t):
+            lo = CHUNK if (k, t, 0) in VIA_GPSIMD else 0
+            if lo < TILES[k][2]:
+                rectify(k, t, lo, TILES[k][2])
+
+
+        def store_y(k, first=0, last=PACK):
+            g, lo, width = TILES[k]
+            rows = out_0[g * SPAN : (g + 1) * SPAN, lo : lo + width].rearrange("(p t) f -> p t f", t=PACK)
+            nc.sync.dma_start(out=rows[:, first:last, :], in_=y[k][:, first:last, :])
+
+        def finish_y(k, slots_a_store):
+            for t in range(PACK):
+                rectify_rest(k, t)
+                if (t + 1) % slots_a_store == 0:
+                    store_y(k, t + 1 - slots_a_store, t + 1)
+
+        def sort_y(k, copy, lo, hi):
+            if k not in y_sorted:
+                y_sorted[k] = stage.tile([P, PACK * TILES[k][2]], BF16, name="y_sorted", align_bytes=64)
             copy(
-                out=y_grouped[k][:].rearrange("p (f t) -> p f t", t=PACK)[:, 2 * lo : 2 * hi],
-                in_=y[k][:].rearrange("p t f -> p f t")[:, 2 * lo : 2 * hi],
+                out=y_sorted[k][:].rearrange("p (f t) -> p f t", t=PACK)[:, lo:hi],
+                in_=y[k][:].rearrange("p t f -> p f t")[:, lo:hi],
             )
 
         def quantize_y(k):
-            g, f0, width = TILES[k]
+            g, first, width = TILES[k]
             y_codes = keep.tile([P, width], U32, name="y_codes_%d" % k, align_bytes=64)
             for lo in range(0, width, CHUNK):
                 nc.vector.quantize_mx(
                     out=y_codes[:, lo : lo + CHUNK].bitcast(FP8X4),
-                    scales=y_scales[4 * g :, f0 + lo : f0 + lo + CHUNK],
-                    in_=y_grouped[k][:, PACK * lo : PACK * (lo + CHUNK)],
+                    scales=y_scales[SCALE_ROWS * g :, first + lo : first + lo + CHUNK],
+                    in_=y_sorted[k][:, PACK * lo : PACK * (lo + CHUNK)],
                 )
             nc.sync.dma_start(
-                out=out_1[g, :, f0 : f0 + width, :].rearrange("p m t -> p (m t)").bitcast(I32),
+                out=out_1[g, :, first : first + width, :].rearrange("p f t -> p (f t)").bitcast(I32),
                 in_=y_codes[:].bitcast(I32),
             )
 
-        def store_scales():
-            for q in range(4):
-                queue = nc.scalar if q % 2 == 0 else nc.sync
-                queue.dma_start(
-                    out=out_2[:, 4 * q : 4 * q + 4, :].bitcast(I32),
-                    in_=y_scales[32 * q : 32 * q + 4 * GROUPS, :].bitcast(I32),
+        def store_scales(lo, hi, queues):
+            for q in range(P // QUADRANT):
+                queues[q % len(queues)].dma_start(
+                    out=out_2[:, SCALE_ROWS * q : SCALE_ROWS * (q + 1), lo:hi].bitcast(I32),
+                    in_=y_scales[QUADRANT * q : QUADRANT * q + SCALE_ROWS * GROUPS, lo:hi].bitcast(I32),
                 )
 
-        banks = [(0, t, 0, BLOCK) for t in range(PACK)] + [(0, t, BLOCK, BLOCK) for t in range(PACK)]
-        for k in range(1, 4):
-            banks.extend([(k, t, lo, CHUNK) for t in range(PACK) for lo in range(0, TILES[k][2], CHUNK)])
-        banks.extend([(4, 0, 0, CHUNK), (5, 0, 0, CHUNK)])
-        banks.extend([(k, t, 0, CHUNK) for k in (4, 5) for t in range(1, PACK)])
-        cursor = {"filled": 0, "read": 0}
 
-        def fill(upto):
-            for i in range(cursor["filled"], min(len(banks), cursor["read"] + AHEAD)):
-                if (banks[i][0], banks[i][2] if banks[i][0] == 0 else 0) > upto:
-                    break
-                multiply(*banks[i])
-                cursor["filled"] = i + 1
-
-        def fill_pass(c):
-            for i in range(cursor["filled"], cursor["filled"] + PACK):
-                multiply(*banks[i], passes=[c])
-            if c == PASSES - 1:
-                cursor["filled"] = cursor["filled"] + PACK
-
-        def empty(count, upto, between=()):
-            for i in range(count):
-                read_acc(*banks[cursor["read"]])
-                cursor["read"] = cursor["read"] + 1
-                fill(upto)
-                if i < len(between):
-                    prepare_x(*between[i])
-
-        def slope_sides(k):
-            if k in SHARED:
-                for lo in range(0, TILES[k][2], CHUNK):
-                    slope_side(k, lo, CHUNK)
-
+        bias = keep.tile([P, GROUPS, PACK], BF16, name="bias")
+        slope_bf16 = keep.tile([P, GROUPS, PACK], BF16, name="slope_bf16")
+        nc.scalar.dma_start(out=slope_bf16[:], in_=slope.rearrange("(g p t) -> p g t", p=P, t=PACK))
+        nc.scalar.dma_start(out=bias[:], in_=prenet_b.rearrange("(g p t) -> p g t", p=P, t=PACK))
         load_w(0, 0)
         load_x(0)
         load_w(1, 0)
-        nc.sync.dma_start(out=bias[:], in_=prenet_b.rearrange("(g p t) -> p g t", p=P, t=PACK))
-        nc.sync.dma_start(out=leak[:], in_=slope.rearrange("(g p t) -> p g t", p=P, t=PACK))
         load_x(1)
-        load_mask(0, 0, 512)
+        load_mask(0, 0, CHUNK)
         load_w(0, 1)
         load_x(2)
         load_w(1, 1)
         load_x(3)
-        load_mask(1, 0, 512)
+        load_mask(1, 0, CHUNK)
         load_x(4)
         load_x(5)
-        load_mask(0, 512, 1536)
-        load_mask(1, 512, 1536)
+        load_mask(0, CHUNK, FRAMES - CHUNK)
+        load_mask(1, CHUNK, FRAMES - CHUNK)
 
+        ident = keep.tile([P, P], F32, name="ident")
         make_identity(nc, ident[:])
-        if SHARED:
-            warm = keep.tile([P, 1], F32, name="warm")
-            nc.scalar.activation(out=warm[:], in_=ident[:, 0:1], func=ACT.Identity)
+        y_scales = keep.tile([P, FRAMES], U8, name="y_scales", align_bytes=64)
 
-        group_w(0, 0, nc.vector.tensor_copy)
+        slope_f32 = keep.tile([P, GROUPS, PACK], F32, name="slope_f32")
+        slope_bias = keep.tile([P, GROUPS, PACK], F32, name="slope_bias")
+        nc.scalar.activation(out=slope_f32[:], in_=slope_bf16[:], func=IDENTITY)
+
+        sort_w(0, 0, nc.vector.tensor_copy)
         quantize_w(0, 0)
-        prepare_x(0, 0)
-        group_w(1, 0, nc.vector.tensor_copy, 0, W_SPLIT)
-        group_w(1, 0, nc.scalar.copy, W_SPLIT, P // 2)
-        prepare_x(0, 1)
-        quantize_x(0, 0, BLOCK)
+        turn_and_sort_x(0, 0)
+        sort_w(1, 0, nc.vector.tensor_copy, 0, HEAD_W_SLOTS)
+        sort_w(1, 0, nc.scalar.copy, HEAD_W_SLOTS, PACK)
+        turn_and_sort_x(0, 1)
+        quantize_block(0, 0)
         quantize_w(1, 0)
-        quantize_x(0, CHUNK, CHUNK + BLOCK)
-        if SHARED:
-            leak_f32 = keep.tile([P, GROUPS], F32, name="leak_f32")
-            leak_bias = keep.tile([P, GROUPS], F32, name="leak_bias")
-            nc.vector.tensor_copy(out=leak_f32[:], in_=leak[:, :, 0])
-            nc.vector.tensor_tensor(out=leak_bias[:], in0=leak[:, :, 0], in1=bias[:, :, 0], op=ALU.mult)
-        prepare_x(1, 0)
-        fill((0, 0))
-        prepare_x(1, 1)
+        quantize_block(0, 1)
+        nc.vector.tensor_tensor(out=slope_bias[:], in0=slope_bf16[:], in1=bias[:], op=ALU.mult)
+        turn_and_sort_x(1, 0)
+        make_products(products_before(0, BLOCK))
+        turn_and_sort_x(1, 1)
         load_x(6)
         load_x(7)
         turn_x(2, 0)
-        group_w(0, 1, nc.scalar.copy)
-        empty(4, (0, 0))
-        quantize_x(0, BLOCK, CHUNK)
+        sort_w(0, 1, nc.scalar.copy)
+        read_products(PACK, products_before(0, BLOCK))
+
+        quantize_block(1, 0)
         rectify(0, 0, 0, BLOCK)
         rectify(0, 1, 0, BLOCK)
-        quantize_x(0, CHUNK + BLOCK, 2 * CHUNK)
-        fill((0, BLOCK))
+        quantize_block(1, 1)
+        make_products(products_before(1))
         rectify(0, 2, 0, BLOCK)
         rectify(0, 3, 0, BLOCK)
+        sort_w(1, 1, nc.scalar.copy, NEXT_W_SLOTS, PACK)
+        sort_x(2, 0)
+        turn_and_sort_x(3, 0)
+        turn_and_sort_x(2, 1)
+        read_products(PACK, products_before(1))
 
-        group_w(1, 1, nc.scalar.copy, W_SPLIT2, P // 2)
-        group_x(2, 0)
-        prepare_x(3, 0)
-        prepare_x(2, 1)
-        empty(4, (0, BLOCK))
-        rectify(0, 0, BLOCK, BLOCK)
+        tile_1 = PRODUCTS[products_before(1) : products_before(2)]
+        rectify(0, 0, BLOCK, CHUNK)
         quantize_w(0, 1)
-        fill_pass(0)
-        group_w(1, 1, nc.vector.tensor_copy, 0, W_SPLIT2)
-        rectify(0, 1, BLOCK, BLOCK)
-        prepare_x(3, 1)
+        for product in tile_1:
+            multiply(*product, 0)
+        sort_w(1, 1, nc.vector.tensor_copy, 0, NEXT_W_SLOTS)
+        rectify(0, 1, BLOCK, CHUNK)
+        turn_and_sort_x(3, 1)
         quantize_w(1, 1)
-        fill_pass(1)
-        slope_sides(1)
-        for t in range(2, PACK):
-            rectify(0, t, BLOCK, BLOCK)
+        for product in tile_1:
+            multiply(*product, 1)
+        count["made"] = products_before(2)
+        rectify(0, 2, BLOCK, CHUNK)
+        rectify(0, 3, BLOCK, CHUNK)
         store_y(0)
-        group_y(0, nc.scalar.copy, 0, CHUNK // 4)
+        sort_y(0, nc.scalar.copy, 0, BLOCK)
+        turn_and_sort_chunk(2)
+        read_products(PACK, products_before(2))
 
-        prepare_x(4, 0)
-        prepare_x(5, 0)
-        prepare_x(4, 1)
-        prepare_x(5, 1)
-        empty(4, (1, 0))
         quantize_x(1)
-        rectify(1, 0)
-        rectify(1, 1)
+        make_products(products_before(2, CHUNK))
+        apply_slope(2)
+        rectify_rest(1, 0)
+        rectify_rest(1, 1)
         quantize_x(2)
-        fill((2, 0))
-        slope_sides(2)
-        group_y(0, nc.scalar.copy, CHUNK // 4, CHUNK // 2)
-        rectify(1, 2)
-        rectify(1, 3)
+        make_products(products_before(3))
+        sort_y(0, nc.scalar.copy, BLOCK, CHUNK)
+        rectify_rest(1, 2)
+        rectify_rest(1, 3)
         store_y(1)
-        group_y(1, nc.scalar.copy)
+        sort_y(1, nc.scalar.copy, 0, CHUNK)
+        read_products(RUN, products_before(4))
 
-        empty(8, (3, 0))
-        slope_sides(3)
-        for b, c in [(6, 0), (7, 0), (6, 1), (7, 1)]:
-            prepare_x(b, c)
+        apply_slope(3)
+        turn_and_sort_chunk(3)
+        free_banks.extend(range(TURN_BANKS))
+        make_products(products_before(4))
         quantize_y(0)
-        for t in range(PACK):
-            rectify(2, t)
-            if t % 2 == 1:
-                store_y(2, t - 1, t + 1)
-            if t == 1:
-                quantize_y(1)
-        group_y(2, nc.scalar.copy)
+        rectify_rest(2, 0)
+        rectify_rest(2, 1)
+        store_y(2, 0, 2)
+        quantize_y(1)
+        rectify_rest(2, 2)
+        rectify_rest(2, 3)
+        store_y(2, 2, PACK)
+        sort_y(2, nc.scalar.copy, 0, 2 * CHUNK)
+        read_products(RUN, products_before(4))
+
         quantize_x(3)
-
-        empty(8, (5, 0))
-        slope_sides(4)
-        slope_sides(5)
-        for t in range(PACK):
-            rectify(3, t)
-            store_y(3, t, t + 1)
+        make_products(len(PRODUCTS))
+        apply_slope(4)
+        finish_y(3, 1)
         quantize_y(2)
-        group_y(3, nc.scalar.copy)
-
-        empty(6, (5, 0))
-        store_y(4, 0, 1)
-        store_y(5, 0, 1)
-        for t in range(1, PACK):
-            rectify(4, t)
-            store_y(4, t, t + 1)
-        group_y(4, nc.scalar.copy)
+        sort_y(3, nc.scalar.copy, 0, 2 * CHUNK)
+        read_products(RUN, len(PRODUCTS))
+        finish_y(4, 2)
+        sort_y(4, nc.scalar.copy, 0, CHUNK)
         quantize_y(3)
-        empty(2, (5, 0))
-        for t in range(1, PACK):
-            rectify(5, t)
-            store_y(5, t, t + 1)
+        store_scales(0, LAST_CHUNK, [nc.sync])
+        finish_y(5, 2)
         quantize_y(4)
-        group_y(5, nc.vector.tensor_copy, 0, Y_SPLIT)
-        group_y(5, nc.scalar.copy, Y_SPLIT, CHUNK // 2)
+        sort_y(5, nc.vector.tensor_copy, 0, TAIL_FRAMES)
+        sort_y(5, nc.scalar.copy, TAIL_FRAMES, CHUNK)
         quantize_y(5)
-        store_scales()
+        store_scales(LAST_CHUNK, FRAMES, [nc.scalar, nc.sync])

from contextlib import ExitStack

import concourse.mybir as mybir
from concourse.masks import make_identity

FRAMES, CH, UNITS = 2048, 1024, 1024
FLOPS = 2 * FRAMES * CH * UNITS

F32 = mybir.dt.float32
BF16 = mybir.dt.bfloat16
I32 = mybir.dt.int32
U32 = mybir.dt.uint32
U8 = mybir.dt.uint8
FP8X4 = mybir.dt.float8_e4m3fn_x4
ALU = mybir.AluOpType
IDENTITY = mybir.ActivationFunctionType.Identity

P = 128
PACK = 4
SPAN = P * PACK
PASSES = CH // SPAN
GROUPS = UNITS // SPAN
CHUNK = 512
BLOCK = 256
QUADRANT = 32
SCALE_ROWS = 4

TILES = [(0, 0, CHUNK), (1, 0, CHUNK), (0, CHUNK, 2 * CHUNK), (1, CHUNK, 2 * CHUNK),
         (0, 3 * CHUNK, CHUNK), (1, 3 * CHUNK, CHUNK)]
LAST_CHUNK = FRAMES - CHUNK

PRODUCTS = [(0, t, lo, BLOCK) for lo in (0, BLOCK) for t in range(PACK)] + [
    (k, t, lo, CHUNK) for k in range(1, len(TILES)) for lo in range(0, TILES[k][2], CHUNK) for t in range(PACK)
]
RUN = 8
GPSIMD_SLOTS = 3
VIA_GPSIMD = [(k, t, 0) for k in (2, 3, 4) for t in range(GPSIMD_SLOTS)]

BANKS = 8
TURN_BANKS = 3

HEAD_W_SLOTS = 3
NEXT_W_SLOTS = 2
TAIL_FRAMES = 320


def tile_vocoder_prenet_units_first_g2_kernel(
    tc, states, prenet_w, prenet_b, slope, drop_mask, out_0, out_1, out_2
):
    nc = tc.nc
    with ExitStack() as ctx:
        keep = ctx.enter_context(tc.tile_pool(name="keep", bufs=1))
        stage = ctx.enter_context(tc.tile_pool(name="stage", bufs=2))
        psum = ctx.enter_context(tc.psum_pool(name="psum", bufs=1))
        ctx.enter_context(tc.manual_schedule())

        w_raw, w_sorted, w_codes, w_scales = {}, {}, {}, {}
        x_raw, x_turned, x_sorted, x_codes, x_scales = {}, {}, {}, {}, {}
        mask, sums, bank_of, sloped, y, y_sorted = {}, {}, {}, {}, {}, {}
        free_banks = list(range(TURN_BANKS, BANKS))
        count = {"made": 0, "read": 0}


        def load_w(c, g):
            w_raw[c, g] = keep.tile([P, PACK, SPAN], BF16, name="w_raw_%d_%d" % (c, g))
            rows = prenet_w[c * SPAN : (c + 1) * SPAN, g * SPAN : (g + 1) * SPAN]
            nc.sync.dma_start(out=w_raw[c, g][:], in_=rows.rearrange("(p j) u -> p j u", j=PACK))

        def load_x(b):
            x_raw[b] = stage.tile([P, 2 * CH], BF16, name="x_raw", bufs=6)
            rows = states[b * BLOCK : (b + 1) * BLOCK, :]
            nc.sync.dma_start(out=x_raw[b][:], in_=rows.rearrange("(r i) k -> r (i k)", i=2))

        def load_mask(g, first, frames):
            held = keep.tile([P, PACK, frames], BF16, name="mask_%d_%d" % (g, first))
            rows = drop_mask[g * SPAN : (g + 1) * SPAN, first : first + frames]
            nc.sync.dma_start(out=held[:], in_=rows.rearrange("(p t) f -> p t f", t=PACK))
            for lo in range(0, frames, CHUNK):
                mask[g, first + lo] = held[:, :, lo : lo + CHUNK]


        def sort_w(c, g, copy, first=0, last=PACK):
            if (c, g) not in w_sorted:
                w_sorted[c, g] = stage.tile([P, PACK * SPAN], BF16, name="w_sorted", align_bytes=64)
            copy(
                out=w_sorted[c, g][:].rearrange("p (t h n j) -> p h t n j", t=PACK, n=2, j=PACK)[:, :, first:last],
                in_=w_raw[c, g][:].rearrange("p j (h n t) -> p h t n j", n=2, t=PACK)[:, :, first:last],
            )

        def quantize_w(c, g):
            w_codes[c, g] = keep.tile([P, SPAN], U32, name="w_codes_%d_%d" % (c, g), align_bytes=64)
            w_scales[c, g] = keep.tile([P, SPAN], U8, name="w_scales_%d_%d" % (c, g), align_bytes=64)
            nc.vector.quantize_mx(
                out=w_codes[c, g][:].bitcast(FP8X4), scales=w_scales[c, g][:], in_=w_sorted[c, g][:]
            )


        def turn_x(b, c):
            bank = len(x_turned) % TURN_BANKS
            x_turned[b, c] = psum.tile([P, 4, P], F32, name="x_turned", tag="bank_%d" % bank)
            pairs = x_raw[b][:].bitcast(F32)
            for i in range(2):
                first = i * (CH // 2) + c * (SPAN // 2)
                for u in range(2):
                    nc.tensor.transpose(
                        x_turned[b, c][:, 2 * i + u, :], pairs[:, first + u : first + SPAN // 2 : 2], ident[:]
                    )

        def sort_x(b, c):
            chunk, half = divmod(b, 2)
            if chunk not in x_sorted:
                x_sorted[chunk] = stage.tile([P, PASSES * PACK * CHUNK], BF16, name="x_sorted", align_bytes=64)
            first = 2 * (c * CHUNK + half * BLOCK)
            pairs = x_sorted[chunk][:].bitcast(F32)[:, first : first + 2 * BLOCK]
            nc.scalar.copy(
                out=pairs.rearrange("p (r q) -> p r q", q=4), in_=x_turned[b, c][:].rearrange("p q r -> p r q")
            )

        def turn_and_sort_x(b, c):
            turn_x(b, c)
            sort_x(b, c)

        def turn_and_sort_chunk(chunk):
            for c in range(PASSES):
                for b in (2 * chunk, 2 * chunk + 1):
                    turn_and_sort_x(b, c)

        def quantize_x(chunk, first=0, words=PASSES * CHUNK):
            if chunk not in x_codes:
                x_codes[chunk] = keep.tile([P, PASSES * CHUNK], U32, name="x_codes_%d" % chunk, align_bytes=64)
                x_scales[chunk] = keep.tile([P, PASSES * CHUNK], U8, name="x_scales_%d" % chunk, align_bytes=64)
            nc.vector.quantize_mx(
                out=x_codes[chunk][:, first : first + words].bitcast(FP8X4),
                scales=x_scales[chunk][:, first : first + words],
                in_=x_sorted[chunk][:, PACK * first : PACK * (first + words)],
            )

        def quantize_block(b, c):
            quantize_x(b // 2, c * CHUNK + (b % 2) * BLOCK, BLOCK)


        def multiply(k, t, lo, frames, c):
            g, first, width = TILES[k]
            chunk, start = divmod(first + lo, CHUNK)
            if c == 0:
                bank_of[k, t, lo] = free_banks.pop(0)
                sums[k, t, lo] = psum.tile([P, frames], F32, name="sums", tag="bank_%d" % bank_of[k, t, lo])
            units = slice(t * P, (t + 1) * P)
            words = slice(c * CHUNK + start, c * CHUNK + start + frames)
            nc.tensor.matmul_mx(
                out=sums[k, t, lo][:],
                lhsT=w_codes[c, g][:, units].bitcast(FP8X4),
                lhsT_scale=w_scales[c, g][:, units],
                rhs=x_codes[chunk][:, words].bitcast(FP8X4),
                rhs_scale=x_scales[chunk][:, words],
                start=(c == 0),
                stop=(c == PASSES - 1),
            )

        def products_before(k, lo=0):
            return PRODUCTS.index((k, 0, lo, BLOCK if k == 0 else CHUNK))

        def make_products(ready):
            for i in range(count["made"], min(ready, count["made"] + len(free_banks))):
                for c in range(PASSES):
                    multiply(*PRODUCTS[i], c)
                count["made"] = i + 1

        def apply_slope(k):
            g = TILES[k][0]
            for t in range(GPSIMD_SLOTS):
                sloped[k, t] = stage.tile([P, CHUNK], F32, name="sloped", bufs=GPSIMD_SLOTS + 1)
                nc.scalar.activation(
                    out=sloped[k, t][:], in_=sums[k, t, 0][:], func=IDENTITY,
                    scale=slope_f32[:, g, t : t + 1], bias=slope_bias[:, g, t : t + 1],
                )

        def read_product(k, t, lo, frames):
            g, first, width = TILES[k]
            if k not in y:
                y[k] = keep.tile([P, PACK, width], F32, name="y_%d" % k)
            start = (first + lo) % CHUNK
            kept = mask[g, first + lo - start][:, t, start : start + frames]
            part = y[k][:, t, lo : lo + frames]
            if (k, t, lo) in VIA_GPSIMD:
                nc.vector.scalar_tensor_tensor(
                    out=sloped[k, t][:], in0=sums[k, t, lo][:], scalar=bias[:, g, t : t + 1], in1=sloped[k, t][:],
                    op0=ALU.add, op1=ALU.max,
                )
                nc.gpsimd.tensor_tensor(out=part, in0=sloped[k, t][:], in1=kept, op=ALU.mult)
            else:
                nc.vector.scalar_tensor_tensor(
                    out=part, in0=sums[k, t, lo][:], scalar=bias[:, g, t : t + 1], in1=kept,
                    op0=ALU.add, op1=ALU.mult,
                )
            free_banks.append(bank_of[k, t, lo])

        def read_products(n, ready):
            for i in range(count["read"], count["read"] + n):
                read_product(*PRODUCTS[i])
                make_products(ready)
            count["read"] = count["read"] + n

        def rectify(k, t, lo, hi):
            part = y[k][:, t, lo:hi]
            nc.vector.scalar_tensor_tensor(
                out=part, in0=part, scalar=slope_bf16[:, TILES[k][0], t : t + 1], in1=part, op0=ALU.mult, op1=ALU.max
            )

        def rectify_rest(k, t):
            lo = CHUNK if (k, t, 0) in VIA_GPSIMD else 0
            if lo < TILES[k][2]:
                rectify(k, t, lo, TILES[k][2])


        def store_y(k, first=0, last=PACK):
            g, lo, width = TILES[k]
            rows = out_0[g * SPAN : (g + 1) * SPAN, lo : lo + width].rearrange("(p t) f -> p t f", t=PACK)
            nc.sync.dma_start(out=rows[:, first:last, :], in_=y[k][:, first:last, :])

        def finish_y(k, slots_a_store):
            for t in range(PACK):
                rectify_rest(k, t)
                if (t + 1) % slots_a_store == 0:
                    store_y(k, t + 1 - slots_a_store, t + 1)

        def sort_y(k, copy, lo, hi):
            if k not in y_sorted:
                y_sorted[k] = stage.tile([P, PACK * TILES[k][2]], BF16, name="y_sorted", align_bytes=64)
            copy(
                out=y_sorted[k][:].rearrange("p (f t) -> p f t", t=PACK)[:, lo:hi],
                in_=y[k][:].rearrange("p t f -> p f t")[:, lo:hi],
            )

        def quantize_y(k):
            g, first, width = TILES[k]
            y_codes = keep.tile([P, width], U32, name="y_codes_%d" % k, align_bytes=64)
            for lo in range(0, width, CHUNK):
                nc.vector.quantize_mx(
                    out=y_codes[:, lo : lo + CHUNK].bitcast(FP8X4),
                    scales=y_scales[SCALE_ROWS * g :, first + lo : first + lo + CHUNK],
                    in_=y_sorted[k][:, PACK * lo : PACK * (lo + CHUNK)],
                )
            nc.sync.dma_start(
                out=out_1[g, :, first : first + width, :].rearrange("p f t -> p (f t)").bitcast(I32),
                in_=y_codes[:].bitcast(I32),
            )

        def store_scales(lo, hi, queues):
            for q in range(P // QUADRANT):
                queues[q % len(queues)].dma_start(
                    out=out_2[:, SCALE_ROWS * q : SCALE_ROWS * (q + 1), lo:hi].bitcast(I32),
                    in_=y_scales[QUADRANT * q : QUADRANT * q + SCALE_ROWS * GROUPS, lo:hi].bitcast(I32),
                )


        bias = keep.tile([P, GROUPS, PACK], BF16, name="bias")
        slope_bf16 = keep.tile([P, GROUPS, PACK], BF16, name="slope_bf16")
        nc.scalar.dma_start(out=slope_bf16[:], in_=slope.rearrange("(g p t) -> p g t", p=P, t=PACK))
        nc.scalar.dma_start(out=bias[:], in_=prenet_b.rearrange("(g p t) -> p g t", p=P, t=PACK))
        load_w(0, 0)
        load_x(0)
        load_w(1, 0)
        load_x(1)
        load_mask(0, 0, CHUNK)
        load_w(0, 1)
        load_x(2)
        load_w(1, 1)
        load_x(3)
        load_mask(1, 0, CHUNK)
        load_x(4)
        load_x(5)
        load_mask(0, CHUNK, FRAMES - CHUNK)
        load_mask(1, CHUNK, FRAMES - CHUNK)

        ident = keep.tile([P, P], F32, name="ident")
        make_identity(nc, ident[:])
        y_scales = keep.tile([P, FRAMES], U8, name="y_scales", align_bytes=64)

        slope_f32 = keep.tile([P, GROUPS, PACK], F32, name="slope_f32")
        slope_bias = keep.tile([P, GROUPS, PACK], F32, name="slope_bias")
        nc.scalar.activation(out=slope_f32[:], in_=slope_bf16[:], func=IDENTITY)

        sort_w(0, 0, nc.vector.tensor_copy)
        quantize_w(0, 0)
        turn_and_sort_x(0, 0)
        sort_w(1, 0, nc.vector.tensor_copy, 0, HEAD_W_SLOTS)
        sort_w(1, 0, nc.scalar.copy, HEAD_W_SLOTS, PACK)
        turn_and_sort_x(0, 1)
        quantize_block(0, 0)
        quantize_w(1, 0)
        quantize_block(0, 1)
        nc.vector.tensor_tensor(out=slope_bias[:], in0=slope_bf16[:], in1=bias[:], op=ALU.mult)
        turn_and_sort_x(1, 0)
        make_products(products_before(0, BLOCK))
        turn_and_sort_x(1, 1)
        load_x(6)
        load_x(7)
        turn_x(2, 0)
        sort_w(0, 1, nc.scalar.copy)
        read_products(PACK, products_before(0, BLOCK))

        quantize_block(1, 0)
        rectify(0, 0, 0, BLOCK)
        rectify(0, 1, 0, BLOCK)
        quantize_block(1, 1)
        make_products(products_before(1))
        rectify(0, 2, 0, BLOCK)
        rectify(0, 3, 0, BLOCK)
        sort_w(1, 1, nc.scalar.copy, NEXT_W_SLOTS, PACK)
        sort_x(2, 0)
        turn_and_sort_x(3, 0)
        turn_and_sort_x(2, 1)
        read_products(PACK, products_before(1))

        tile_1 = PRODUCTS[products_before(1) : products_before(2)]
        rectify(0, 0, BLOCK, CHUNK)
        quantize_w(0, 1)
        for product in tile_1:
            multiply(*product, 0)
        sort_w(1, 1, nc.vector.tensor_copy, 0, NEXT_W_SLOTS)
        rectify(0, 1, BLOCK, CHUNK)
        turn_and_sort_x(3, 1)
        quantize_w(1, 1)
        for product in tile_1:
            multiply(*product, 1)
        count["made"] = products_before(2)
        rectify(0, 2, BLOCK, CHUNK)
        rectify(0, 3, BLOCK, CHUNK)
        store_y(0)
        sort_y(0, nc.scalar.copy, 0, BLOCK)
        turn_and_sort_chunk(2)
        read_products(PACK, products_before(2))

        quantize_x(1)
        make_products(products_before(2, CHUNK))
        apply_slope(2)
        rectify_rest(1, 0)
        rectify_rest(1, 1)
        quantize_x(2)
        make_products(products_before(3))
        sort_y(0, nc.scalar.copy, BLOCK, CHUNK)
        rectify_rest(1, 2)
        rectify_rest(1, 3)
        store_y(1)
        sort_y(1, nc.scalar.copy, 0, CHUNK)
        read_products(RUN, products_before(4))

        apply_slope(3)
        turn_and_sort_chunk(3)
        free_banks.extend(range(TURN_BANKS))
        make_products(products_before(4))
        quantize_y(0)
        rectify_rest(2, 0)
        rectify_rest(2, 1)
        store_y(2, 0, 2)
        quantize_y(1)
        rectify_rest(2, 2)
        rectify_rest(2, 3)
        store_y(2, 2, PACK)
        sort_y(2, nc.scalar.copy, 0, 2 * CHUNK)
        read_products(RUN, products_before(4))

        quantize_x(3)
        make_products(len(PRODUCTS))
        apply_slope(4)
        finish_y(3, 1)
        quantize_y(2)
        sort_y(3, nc.scalar.copy, 0, 2 * CHUNK)
        read_products(RUN, len(PRODUCTS))
        finish_y(4, 2)
        sort_y(4, nc.scalar.copy, 0, CHUNK)
        quantize_y(3)
        store_scales(0, LAST_CHUNK, [nc.sync])
        finish_y(5, 2)
        quantize_y(4)
        sort_y(5, nc.vector.tensor_copy, 0, TAIL_FRAMES)
        sort_y(5, nc.scalar.copy, TAIL_FRAMES, CHUNK)
        quantize_y(5)
        store_scales(LAST_CHUNK, FRAMES, [nc.scalar, nc.sync])
